import numpy as np
import ml_dtypes


def mxq(x, axis, fmt="e4m3"):
    dtype, down = {"e4m3": (ml_dtypes.float8_e4m3fn, 7), "e5m2": (ml_dtypes.float8_e5m2, 14)}[fmt]
    v = np.moveaxis(np.asarray(x, np.float32).astype(ml_dtypes.bfloat16).astype(np.float64), axis, -1)
    blocks = v.reshape(v.shape[:-1] + (-1, 32))
    amax = np.abs(blocks).max(-1, keepdims=True)
    byte = np.maximum(np.where(amax > 0, np.frexp(amax)[1] - 1 + 127, 0) - down, 1)
    scale = np.exp2(byte - 127.0)
    codes = (blocks / scale).astype(np.float32).astype(dtype).astype(np.float64)
    return np.moveaxis((codes * scale).reshape(v.shape), -1, axis)


WIDE = False


def mx_kscale(k):
    if not WIDE:
        return np.ones(k)
    levels = np.array([10, -10, 5, -5, 0])
    if k % 512:
        return np.exp2(np.random.permutation(np.resize(levels, k // 32))).repeat(32)
    a = np.empty((k // 512, 16))
    for p in range(k // 512):
        a[p, :8] = np.random.permutation(np.resize(levels, 8))
        for g in range(8):
            far = levels[np.abs(levels - a[p, g]) >= 10]
            a[p, g + 8] = far[np.random.randint(len(far))]
    return np.exp2(a.ravel()).repeat(32)


def f64(x):
    return np.asarray(x).astype(np.float64)


def striped(idx):
    return np.tile(idx.reshape(-1, 16).T, (8, 1)).astype(np.uint16)


def unstriped(offs):
    return offs[:16].T.reshape(-1).astype(np.int64)


def striped8(idx):
    return np.concatenate([x.reshape(-1, 16).T for x in idx]).astype(np.uint16)


def runs(offs, k):
    lists = np.stack([offs[16 * r : 16 * r + 16].T.reshape(-1) for r in range(8)]).astype(np.int64)
    return lists[np.arange(k) % 512 // 64]


def pack_weight(w):
    k, n = w.shape
    w = f64(np.asarray(w, np.float32).astype(ml_dtypes.bfloat16)).reshape(k // 32, 32, n)
    amax = np.abs(w).max(1)
    byte = np.clip(np.where(amax > 0, np.frexp(amax)[1] - 1 + 127 - 7, 1), 1, 254)
    scaled = (w * np.exp2(127.0 - byte)[:, None, :]).reshape(k, n).astype(np.float32)
    words = np.ascontiguousarray(scaled.reshape(k // 512, 128, 4, n).transpose(0, 1, 3, 2)).astype(ml_dtypes.float8_e4m3fn).view(np.uint8)
    return words, np.ascontiguousarray(byte.astype(np.uint8).reshape(k // 512, 16, n))


def unpack_weight(words, scales):
    g, p, n, _ = words.shape
    vals = np.ascontiguousarray(words).view(ml_dtypes.float8_e4m3fn).astype(np.float64) * np.repeat(np.exp2(scales.astype(np.float64) - 127.0), 8, axis=1)[..., None]
    return vals.transpose(0, 1, 3, 2).reshape(g * 512, n)


E2M1 = np.array([0.0, 0.5, 1.0, 1.5, 2.0, 3.0, 4.0, 6.0, -0.0, -0.5, -1.0, -1.5, -2.0, -3.0, -4.0, -6.0])


def pack_fp4(w):
    k, n = w.shape
    w = f64(np.asarray(w, np.float32).astype(ml_dtypes.bfloat16)).reshape(k // 32, 32, n)
    amax = np.abs(w).max(1)
    mant, ex = np.frexp(amax / 6.0)
    byte = np.clip(np.where(amax > 0, np.where(mant > 0.5, ex, ex - 1) + 127, 1), 1, 254)
    scaled = (w * np.exp2(127.0 - byte)[:, None, :]).reshape(k, n).astype(np.float32)
    c = np.ascontiguousarray(scaled.reshape(k // 512, 128, 4, n).transpose(0, 1, 3, 2)).astype(ml_dtypes.float4_e2m1fn).view(np.uint8) & 0xF
    words = (c[..., 0::2] | (c[..., 1::2] << 4)).reshape(k // 512, 128, 2 * n)
    return np.ascontiguousarray(words), np.ascontiguousarray(byte.astype(np.uint8).reshape(k // 512, 16, n))


def unpack_fp4(words, scales):
    g, _, n = scales.shape
    words = np.ascontiguousarray(words).reshape(g, 128, n, 2)
    nib = np.empty((g, 128, n, 4), np.uint8)
    nib[..., 0::2] = words & 0xF
    nib[..., 1::2] = words >> 4
    vals = E2M1[nib] * np.repeat(np.exp2(scales.astype(np.float64) - 127.0), 8, axis=1)[..., None]
    return vals.transpose(0, 1, 3, 2).reshape(g * 512, n)


def planes(y):
    n, m = y.shape
    v = y.astype(np.float32).astype(ml_dtypes.bfloat16).astype(np.float64).reshape(n // 32, 32, m)
    top = np.abs(v).max(1)
    byte = np.clip(np.where(top > 0, np.frexp(top)[1] - 1 + 127 - 7, 1), 1, 254)
    codes = (v * np.exp2(127.0 - byte)[:, None, :]).reshape(n, m).astype(np.float32).astype(ml_dtypes.float8_e4m3fn).view(np.uint8)
    words = codes.reshape(n // 512, 128, 4, m).transpose(0, 1, 3, 2)
    return np.ascontiguousarray(words), np.ascontiguousarray(byte.astype(np.uint8).reshape(n // 512, 16, m))


K, T, S, H, G = 512, 2048, 512, 512, 2048


def setup_inputs():
    n = np.random.standard_normal
    s = mx_kscale(K)[:, None]
    packed_xT = pack_weight(n((K, T)) * s)
    packed_w1 = pack_fp4(n((K, H)) / np.sqrt(K) / s)
    packed_dT = pack_weight(n((K, G)) / s)
    return {
        "x_words": packed_xT[0],
        "x_scales": packed_xT[1],
        "w1_words": packed_w1[0],
        "w1_scales": packed_w1[1],
        "gs": (np.random.uniform(0.5, 1.5, (K, 1)) * s).astype(np.float32),
        "d_words": packed_dT[0],
        "d_scales": packed_dT[1],
        "offs": striped(np.random.permutation(T)[:S]),
        "n1": striped8(np.stack([np.random.permutation(S) for _ in range(8)])),
        "n2": striped8(np.stack([np.random.permutation(S) for _ in range(8)])),
        "k1": striped8(np.random.randint(0, G, (8, H))),
        "n3": striped8(np.stack([np.random.permutation(S) for _ in range(8)])),
        "n4": striped8(np.stack([np.random.permutation(S) for _ in range(8)])),
    }


def reference(x_words, x_scales, w1_words, w1_scales, gs, d_words, d_scales, offs, n1, n2, k1, n3, n4):
    d_k1 = unpack_weight(d_words, d_scales)[np.arange(K)[:, None], runs(k1, K)]
    xq = unpack_weight(x_words, x_scales)[:, unstriped(offs)]
    y = unpack_fp4(w1_words, w1_scales).T @ xq
    z = f64(gs) * (y[np.arange(H)[:, None], runs(n1, H)] + 0.75 * (y[np.arange(H)[:, None], runs(n2, H)]))
    h = 0.0625 * ((d_k1.T @ mxq(z, 0, "e4m3")))
    st = h - (h[np.arange(H)[:, None], runs(n3, H)])
    out_0 = np.maximum(st, st[np.arange(H)[:, None], runs(n4, H)])
    return (out_0,) + planes(out_0)

@@ -1,0 +1,213 @@
+from contextlib import ExitStack
+
+import concourse.mybir as mybir
+
+K, T, S, H, G = 512, 2048, 512, 512, 2048
+FLOPS = 2 * K * H * S + 2 * H * H * S
+
+F32 = mybir.dt.float32
+BF16 = mybir.dt.bfloat16
+I32 = mybir.dt.int32
+U32 = mybir.dt.uint32
+U16 = mybir.dt.uint16
+U8 = mybir.dt.uint8
+FP8X4 = mybir.dt.float8_e4m3fn_x4
+FP4X4 = mybir.dt.float4_e2m1fn_x4
+MULT = mybir.AluOpType.mult
+ADD = mybir.AluOpType.add
+MAX = mybir.AluOpType.max
+COPY = mybir.ActivationFunctionType.Copy
+
+P = 128
+PACK = 4
+HALVES = ((0, 256), (256, 512))
+OUT_PIECES = ((0, 256), (256, 384), (384, 512))
+
+
+def entries(offsets, c0, c1):
+    return offsets[:, c0 // 16 : c1 // 16]
+
+
+def interleave(copy, dst, src):
+    copy(dst[:].rearrange("p (c i t) -> p c t i", i=4, t=PACK), src[:].rearrange("p t (c i) -> p c t i", i=4))
+
+
+def tile_picked_densesumhopmx_none_po_kernel(
+    tc, x_words, x_scales, w1_words, w1_scales, gs, d_words, d_scales, offs, n1, n2, k1, n3, n4, out_0, out_1, out_2
+):
+    nc = tc.nc
+    with ExitStack() as ctx:
+        lists = ctx.enter_context(tc.tile_pool(name="lists", bufs=1))
+        sb = ctx.enter_context(tc.tile_pool(name="sb", bufs=1))
+        psum = ctx.enter_context(tc.psum_pool(name="psum", bufs=1))
+
+        def tile(shape, dtype, name, tag=None):
+            return sb.tile(shape, dtype, name=name, tag=tag or name, align_bytes=64)
+
+        def load_list(src, name):
+            offsets = lists.tile([P, S // 16], U16, name=name)
+            nc.sync.dma_start(offsets[:], src)
+            return offsets
+
+        xs_table = tile([P, T], U8, "xs_table")
+        w1s_raw = tile([P, H], U8, "w1s_raw")
+        ds_table = tile([P, G], U8, "ds_table")
+        ds_placed = tile([P, H], U8, "ds_placed")
+        nc.vector.memset(xs_table[:].bitcast(I32), 0)
+        nc.vector.memset(w1s_raw[:].bitcast(I32), 0)
+        nc.gpsimd.memset(ds_table[:].bitcast(I32), 0)
+        nc.gpsimd.memset(ds_placed[:].bitcast(I32), 0)
+
+        xw_table = tile([P, T], I32, "xw_table")
+        nc.scalar.dma_start(xw_table[:], x_words[0].rearrange("p n t -> p (n t)").bitcast(I32))
+        offs_sb = load_list(offs, "offs_sb")
+        w1w_raw = tile([P, 2 * H], U8, "w1w_raw")
+        nc.sync.dma_start(w1w_raw[:].bitcast(I32), w1_words[0].bitcast(I32))
+        for q in range(4):
+            nc.sync.dma_start(xs_table[32 * q : 32 * q + 4, :].bitcast(I32), x_scales[0, 4 * q : 4 * q + 4, :].bitcast(I32))
+        for q in range(4):
+            nc.sync.dma_start(w1s_raw[32 * q : 32 * q + 4, :].bitcast(I32), w1_scales[0, 4 * q : 4 * q + 4, :].bitcast(I32))
+        k1_sb = load_list(k1, "k1_sb")
+        for e in range(2):
+            nc.sync.dma_start(ds_table[e:P:16, :].bitcast(I32), d_scales[0, e:16:2, :].bitcast(I32))
+        gs_sb = tile([P, PACK], F32, "gs_sb")
+        nc.sync.dma_start(gs_sb[:], gs.rearrange("(p t) o -> p (t o)", t=PACK))
+        n2_sb = load_list(n2, "n2_sb")
+        n1_sb = load_list(n1, "n1_sb")
+        n3_sb = load_list(n3, "n3_sb")
+        n4_sb = load_list(n4, "n4_sb")
+        dw_table = tile([P, G], I32, "dw_table")
+        nc.sync.dma_start(dw_table[:], d_words[0].rearrange("p n t -> p (n t)").bitcast(I32))
+
+        w1w = tile([P, 2 * H], U8, "w1w")
+        nc.vector.tensor_copy(
+            w1w[:].rearrange("p (t m b) -> p t m b", t=PACK, b=2), w1w_raw[:].rearrange("p (m t b) -> p t m b", t=PACK, b=2)
+        )
+        xs = tile([P, S], U8, "xs")
+        nc.vector.tensor_copy(xs[:], xs_table[:].indirect(offs_sb[:]))
+        xw = tile([P, S], U32, "xw")
+        nc.vector.tensor_copy(xw[:], xw_table[:].bitcast(U32).indirect(offs_sb[:]))
+        w1s = tile([P, H], U8, "w1s")
+        nc.vector.tensor_copy(w1s[:].rearrange("p (t m) -> p t m", t=PACK), w1s_raw[:].rearrange("p (m t) -> p t m", t=PACK))
+
+        gy = []
+        for t in range(PACK):
+            y_ps = psum.tile([P, S], F32, name=f"y_ps{t}", tag=f"bank{t}")
+            nc.tensor.matmul_mx(
+                y_ps[:],
+                lhsT=w1w[:, 2 * P * t : 2 * P * (t + 1)].bitcast(FP4X4),
+                lhsT_scale=w1s[:, P * t : P * (t + 1)],
+                rhs=xw[:].bitcast(FP8X4),
+                rhs_scale=xs[:],
+                start=True,
+                stop=True,
+            )
+            gy_t = tile([P, S], F32, f"gy{t}")
+            nc.scalar.activation(gy_t[:], y_ps[:], COPY, scale=gs_sb[:, t : t + 1])
+            gy.append(gy_t)
+
+        ds_picked = tile([P, H], U8, "ds_picked", tag="xw_table")
+        nc.vector.tensor_copy(ds_picked[:], ds_table[:].indirect(k1_sb[:]))
+        ds_dealt = tile([P, H], U8, "ds_dealt")
+        nc.vector.tensor_copy(
+            ds_dealt[:].rearrange("p (t m) -> p t m", t=PACK), ds_picked[:].rearrange("p (m t) -> p t m", t=PACK)
+        )
+        for odd in range(2):
+            for e in range(2):
+                nc.sync.dma_start(ds_placed[2 * odd + e : P : 32, :].bitcast(I32), ds_dealt[16 * odd + e : P : 32, :].bitcast(I32))
+
+        zw = tile([P, S], U32, "zw")
+        zs = tile([P, S], U8, "zs")
+        second = tile([P, 2, 256], F32, "second")
+        z16 = []
+        for i, (c0, c1) in enumerate(HALVES):
+            z = tile([P, PACK, c1 - c0], F32, f"z{i}")
+            for step in range(PACK + 1):
+                if step < PACK:
+                    nc.vector.tensor_scalar(
+                        second[:, step % 2, :], gy[step][:].indirect(entries(n2_sb, c0, c1)), 0.75, 0.0, MULT, ADD
+                    )
+                if step > 0:
+                    t = step - 1
+                    nc.vector.tensor_tensor(z[:, t, :], gy[t][:].indirect(entries(n1_sb, c0, c1)), second[:, t % 2, :], ADD)
+            z16_i = tile([P, PACK * (c1 - c0)], BF16, f"z16_{i}")
+            interleave(nc.scalar.copy, z16_i, z)
+            z16.append(z16_i)
+
+        def quantize_z(i):
+            c0, c1 = HALVES[i]
+            nc.vector.quantize_mx(zw[:, c0:c1].bitcast(FP8X4), zs[:, c0:c1], z16[i][:])
+
+        quantize_z(0)
+        dw_picked = tile([P, H], U32, "dw_picked", tag="second")
+        nc.vector.tensor_copy(dw_picked[:], dw_table[:].bitcast(U32).indirect(k1_sb[:]))
+        dw_view = dw_picked[:].bitcast(I32).rearrange("p (m t) -> p t m", t=PACK)
+        dw_first = tile([P, P], I32, "dw_first")
+        nc.vector.tensor_copy(dw_first[:], dw_view[:, 0, :])
+        quantize_z(1)
+        dw_rest = tile([P, PACK - 1, P], I32, "dw_rest", tag="z16_1")
+        for t in range(1, PACK):
+            nc.vector.tensor_copy(dw_rest[:, t - 1, :], dw_view[:, t, :])
+
+        out_rows = out_0.rearrange("(p t) c -> p t c", t=PACK)
+        out_words = out_1[0].rearrange("p m t -> p (m t)").bitcast(I32)
+        out_scales = tile([P, S], U8, "out_scales")
+        fetched = tile([P, 2, 256], F32, "fetched")
+        o = [tile([P, PACK, c1 - c0], F32, f"o{i}") for i, (c0, c1) in enumerate(OUT_PIECES)]
+        st = []
+
+        def fetch(i, t):
+            c0, c1 = OUT_PIECES[i]
+            nc.vector.tensor_copy(fetched[:, t % 2, : c1 - c0], st[t][:].indirect(entries(n4_sb, c0, c1)))
+
+        def larger(i, t):
+            c0, c1 = OUT_PIECES[i]
+            nc.vector.tensor_tensor(o[i][:, t, :], st[t][:, c0:c1], fetched[:, t % 2, : c1 - c0], MAX)
+
+        def hand_out(i, copy, queue):
+            c0, c1 = OUT_PIECES[i]
+            nc.sync.dma_start(out_rows[:, :, c0:c1], o[i][:])
+            o16 = tile([P, PACK * (c1 - c0)], BF16, f"o16_{i}")
+            interleave(copy, o16, o[i])
+            words = tile([P, c1 - c0], I32, f"words{i}")
+            nc.vector.quantize_mx(words[:].bitcast(FP8X4), out_scales[:, c0:c1], o16[:])
+            queue.dma_start(out_words[:, c0:c1], words[:])
+
+        for t in range(PACK):
+            dw_t = dw_first[:] if t == 0 else dw_rest[:, t - 1, :]
+            h_neg = tile([P, S], F32, f"h_neg{t}")
+            h_pos = tile([P, S], F32, f"h_pos{t}")
+            for i, (c0, c1) in enumerate(HALVES):
+                h_ps = psum.tile([P, c1 - c0], F32, name=f"h_ps{t}_{i}", tag=f"bank{t + PACK * (1 - i)}")
+                nc.tensor.matmul_mx(
+                    h_ps[:],
+                    lhsT=dw_t.bitcast(FP8X4),
+                    lhsT_scale=ds_placed[:, P * t : P * (t + 1)],
+                    rhs=zw[:, c0:c1].bitcast(FP8X4),
+                    rhs_scale=zs[:, c0:c1],
+                    start=True,
+                    stop=True,
+                )
+                nc.scalar.activation(h_neg[:, c0:c1], h_ps[:], COPY, scale=-0.0625)
+                nc.scalar.activation(h_pos[:, c0:c1], h_ps[:], COPY, scale=0.0625)
+            st_t = tile([P, S], F32, f"st{t}")
+            st.append(st_t)
+            for i, (c0, c1) in enumerate(HALVES):
+                nc.vector.tensor_tensor(st_t[:, c0:c1], h_neg[:].indirect(entries(n3_sb, c0, c1)), h_pos[:, c0:c1], ADD)
+                if i == 0 and t > 0:
+                    larger(0, t - 1)
+            fetch(0, t)
+        for i in range(1, len(OUT_PIECES)):
+            for t in range(PACK):
+                fetch(i, t)
+                if t == 0:
+                    larger(i - 1, PACK - 1)
+                    hand_out(i - 1, nc.scalar.copy, nc.sync)
+                else:
+                    larger(i, t - 1)
+        last = len(OUT_PIECES) - 1
+        larger(last, PACK - 1)
+        hand_out(last, nc.vector.tensor_copy, nc.scalar)
+        for q in range(4):
+            queue = nc.scalar if q % 2 else nc.sync
+            queue.dma_start(out_2[0, 4 * q : 4 * q + 4, :].bitcast(I32), out_scales[32 * q : 32 * q + 4, :].bitcast(I32))

@@ -21,7 +21,6 @@ COPY = mybir.ActivationFunctionType.Copy
 P = 128
 PACK = 4
 HALVES = ((0, 256), (256, 512))
-OUT_PIECES = ((0, 256), (256, 384), (384, 512))
 
 
 def entries(offsets, c0, c1):
@@ -29,7 +28,7 @@ def entries(offsets, c0, c1):
 
 
 def interleave(copy, dst, src):
-    copy(dst[:].rearrange("p (c i t) -> p c t i", i=4, t=PACK), src[:].rearrange("p t (c i) -> p c t i", i=4))
+    copy(dst.rearrange("p (c i t) -> p c t i", i=4, t=PACK), src.rearrange("p t (c i) -> p c t i", i=4))
 
 
 def tile_picked_densesumhopmx_none_po_kernel(
@@ -53,31 +52,35 @@ def tile_picked_densesumhopmx_none_po_kernel(
         w1s_raw = tile([P, H], U8, "w1s_raw")
         ds_table = tile([P, G], U8, "ds_table")
         ds_placed = tile([P, H], U8, "ds_placed")
+        rows = [tile([P, 2 * S], F32, f"rows{t}") for t in range(PACK)]
         nc.vector.memset(xs_table[:].bitcast(I32), 0)
         nc.vector.memset(w1s_raw[:].bitcast(I32), 0)
-        nc.gpsimd.memset(ds_table[:].bitcast(I32), 0)
-        nc.gpsimd.memset(ds_placed[:].bitcast(I32), 0)
+        nc.vector.memset(ds_table[:].bitcast(I32), 0)
+        for t in range(2):
+            nc.vector.memset(rows[t][:, S:], 0.0)
 
-        xw_table = tile([P, T], I32, "xw_table")
-        nc.scalar.dma_start(xw_table[:], x_words[0].rearrange("p n t -> p (n t)").bitcast(I32))
         offs_sb = load_list(offs, "offs_sb")
         w1w_raw = tile([P, 2 * H], U8, "w1w_raw")
         nc.sync.dma_start(w1w_raw[:].bitcast(I32), w1_words[0].bitcast(I32))
-        for q in range(4):
-            nc.sync.dma_start(xs_table[32 * q : 32 * q + 4, :].bitcast(I32), x_scales[0, 4 * q : 4 * q + 4, :].bitcast(I32))
-        for q in range(4):
-            nc.sync.dma_start(w1s_raw[32 * q : 32 * q + 4, :].bitcast(I32), w1_scales[0, 4 * q : 4 * q + 4, :].bitcast(I32))
         k1_sb = load_list(k1, "k1_sb")
+        xw_table = tile([P, T], I32, "xw_table")
+        nc.sync.dma_start(xw_table[:], x_words[0].rearrange("p n t -> p (n t)").bitcast(I32))
+        gs_sb = tile([P, PACK], F32, "gs_sb")
+        nc.gpsimd.dma_start(gs_sb[:], gs.rearrange("(p t) o -> p (t o)", t=PACK))
+        for q in range(4):
+            nc.scalar.dma_start(xs_table[32 * q : 32 * q + 4, :].bitcast(I32), x_scales[0, 4 * q : 4 * q + 4, :].bitcast(I32))
+        for q in range(4):
+            queue = nc.scalar if q < 3 else nc.gpsimd
+            queue.dma_start(w1s_raw[32 * q : 32 * q + 4, :].bitcast(I32), w1_scales[0, 4 * q : 4 * q + 4, :].bitcast(I32))
+        for t in range(2, PACK):
+            nc.gpsimd.memset(rows[t][:, S:], 0.0)
+        nc.gpsimd.memset(ds_placed[:].bitcast(I32), 0)
         for e in range(2):
             nc.sync.dma_start(ds_table[e:P:16, :].bitcast(I32), d_scales[0, e:16:2, :].bitcast(I32))
-        gs_sb = tile([P, PACK], F32, "gs_sb")
-        nc.sync.dma_start(gs_sb[:], gs.rearrange("(p t) o -> p (t o)", t=PACK))
         n2_sb = load_list(n2, "n2_sb")
         n1_sb = load_list(n1, "n1_sb")
         n3_sb = load_list(n3, "n3_sb")
         n4_sb = load_list(n4, "n4_sb")
-        dw_table = tile([P, G], I32, "dw_table")
-        nc.sync.dma_start(dw_table[:], d_words[0].rearrange("p n t -> p (n t)").bitcast(I32))
 
         w1w = tile([P, 2 * H], U8, "w1w")
         nc.vector.tensor_copy(
@@ -85,12 +88,13 @@ def tile_picked_densesumhopmx_none_po_kernel(
         )
         xs = tile([P, S], U8, "xs")
         nc.vector.tensor_copy(xs[:], xs_table[:].indirect(offs_sb[:]))
+        dw_table = tile([P, G], I32, "dw_table", tag="xs_table")
+        nc.sync.dma_start(dw_table[:], d_words[0].rearrange("p n t -> p (n t)").bitcast(I32))
         xw = tile([P, S], U32, "xw")
         nc.vector.tensor_copy(xw[:], xw_table[:].bitcast(U32).indirect(offs_sb[:]))
         w1s = tile([P, H], U8, "w1s")
         nc.vector.tensor_copy(w1s[:].rearrange("p (t m) -> p t m", t=PACK), w1s_raw[:].rearrange("p (m t) -> p t m", t=PACK))
 
-        gy = []
         for t in range(PACK):
             y_ps = psum.tile([P, S], F32, name=f"y_ps{t}", tag=f"bank{t}")
             nc.tensor.matmul_mx(
@@ -102,9 +106,7 @@ def tile_picked_densesumhopmx_none_po_kernel(
                 start=True,
                 stop=True,
             )
-            gy_t = tile([P, S], F32, f"gy{t}")
-            nc.scalar.activation(gy_t[:], y_ps[:], COPY, scale=gs_sb[:, t : t + 1])
-            gy.append(gy_t)
+            nc.scalar.activation(rows[t][:, :S], y_ps[:], COPY, scale=gs_sb[:, t : t + 1])
 
         ds_picked = tile([P, H], U8, "ds_picked", tag="xw_table")
         nc.vector.tensor_copy(ds_picked[:], ds_table[:].indirect(k1_sb[:]))
@@ -118,29 +120,35 @@ def tile_picked_densesumhopmx_none_po_kernel(
 
         zw = tile([P, S], U32, "zw")
         zs = tile([P, S], U8, "zs")
-        second = tile([P, 2, 256], F32, "second")
+        second = tile([P, 2, S], F32, "second")
+        z = tile([P, PACK, S], F32, "z")
+
+        def fetch_second(t, c0, c1):
+            nc.vector.tensor_scalar(second[:, t % 2, c0:c1], rows[t][:].indirect(entries(n2_sb, c0, c1)), 0.75, 0.0, MULT, ADD)
+
+        def add_first(t, c0, c1):
+            nc.vector.tensor_tensor(z[:, t, c0:c1], rows[t][:].indirect(entries(n1_sb, c0, c1)), second[:, t % 2, c0:c1], ADD)
+
+        fetch_second(0, 0, S)
+        for t in range(2):
+            fetch_second(t + 1, 0, S)
+            add_first(t, 0, S)
         z16 = []
         for i, (c0, c1) in enumerate(HALVES):
-            z = tile([P, PACK, c1 - c0], F32, f"z{i}")
-            for step in range(PACK + 1):
-                if step < PACK:
-                    nc.vector.tensor_scalar(
-                        second[:, step % 2, :], gy[step][:].indirect(entries(n2_sb, c0, c1)), 0.75, 0.0, MULT, ADD
-                    )
-                if step > 0:
-                    t = step - 1
-                    nc.vector.tensor_tensor(z[:, t, :], gy[t][:].indirect(entries(n1_sb, c0, c1)), second[:, t % 2, :], ADD)
+            fetch_second(3, c0, c1)
+            add_first(2, c0, c1)
+            add_first(3, c0, c1)
             z16_i = tile([P, PACK * (c1 - c0)], BF16, f"z16_{i}")
-            interleave(nc.scalar.copy, z16_i, z)
+            interleave(nc.scalar.copy, z16_i[:], z[:, :, c0:c1])
             z16.append(z16_i)
 
         def quantize_z(i):
             c0, c1 = HALVES[i]
             nc.vector.quantize_mx(zw[:, c0:c1].bitcast(FP8X4), zs[:, c0:c1], z16[i][:])
 
-        quantize_z(0)
         dw_picked = tile([P, H], U32, "dw_picked", tag="second")
         nc.vector.tensor_copy(dw_picked[:], dw_table[:].bitcast(U32).indirect(k1_sb[:]))
+        quantize_z(0)
         dw_view = dw_picked[:].bitcast(I32).rearrange("p (m t) -> p t m", t=PACK)
         dw_first = tile([P, P], I32, "dw_first")
         nc.vector.tensor_copy(dw_first[:], dw_view[:, 0, :])
@@ -149,34 +157,11 @@ def tile_picked_densesumhopmx_none_po_kernel(
         for t in range(1, PACK):
             nc.vector.tensor_copy(dw_rest[:, t - 1, :], dw_view[:, t, :])
 
-        out_rows = out_0.rearrange("(p t) c -> p t c", t=PACK)
-        out_words = out_1[0].rearrange("p m t -> p (m t)").bitcast(I32)
-        out_scales = tile([P, S], U8, "out_scales")
-        fetched = tile([P, 2, 256], F32, "fetched")
-        o = [tile([P, PACK, c1 - c0], F32, f"o{i}") for i, (c0, c1) in enumerate(OUT_PIECES)]
         st = []
-
-        def fetch(i, t):
-            c0, c1 = OUT_PIECES[i]
-            nc.vector.tensor_copy(fetched[:, t % 2, : c1 - c0], st[t][:].indirect(entries(n4_sb, c0, c1)))
-
-        def larger(i, t):
-            c0, c1 = OUT_PIECES[i]
-            nc.vector.tensor_tensor(o[i][:, t, :], st[t][:, c0:c1], fetched[:, t % 2, : c1 - c0], MAX)
-
-        def hand_out(i, copy, queue):
-            c0, c1 = OUT_PIECES[i]
-            nc.sync.dma_start(out_rows[:, :, c0:c1], o[i][:])
-            o16 = tile([P, PACK * (c1 - c0)], BF16, f"o16_{i}")
-            interleave(copy, o16, o[i])
-            words = tile([P, c1 - c0], I32, f"words{i}")
-            nc.vector.quantize_mx(words[:].bitcast(FP8X4), out_scales[:, c0:c1], o16[:])
-            queue.dma_start(out_words[:, c0:c1], words[:])
-
         for t in range(PACK):
             dw_t = dw_first[:] if t == 0 else dw_rest[:, t - 1, :]
-            h_neg = tile([P, S], F32, f"h_neg{t}")
-            h_pos = tile([P, S], F32, f"h_pos{t}")
+            st_t = tile([P, 2 * S], F32, f"st{t}")
+            st.append(st_t)
             for i, (c0, c1) in enumerate(HALVES):
                 h_ps = psum.tile([P, c1 - c0], F32, name=f"h_ps{t}_{i}", tag=f"bank{t + PACK * (1 - i)}")
                 nc.tensor.matmul_mx(
@@ -188,26 +173,56 @@ def tile_picked_densesumhopmx_none_po_kernel(
                     start=True,
                     stop=True,
                 )
-                nc.scalar.activation(h_neg[:, c0:c1], h_ps[:], COPY, scale=-0.0625)
-                nc.scalar.activation(h_pos[:, c0:c1], h_ps[:], COPY, scale=0.0625)
-            st_t = tile([P, S], F32, f"st{t}")
-            st.append(st_t)
-            for i, (c0, c1) in enumerate(HALVES):
-                nc.vector.tensor_tensor(st_t[:, c0:c1], h_neg[:].indirect(entries(n3_sb, c0, c1)), h_pos[:, c0:c1], ADD)
-                if i == 0 and t > 0:
-                    larger(0, t - 1)
-            fetch(0, t)
-        for i in range(1, len(OUT_PIECES)):
-            for t in range(PACK):
-                fetch(i, t)
-                if t == 0:
-                    larger(i - 1, PACK - 1)
-                    hand_out(i - 1, nc.scalar.copy, nc.sync)
-                else:
-                    larger(i, t - 1)
-        last = len(OUT_PIECES) - 1
-        larger(last, PACK - 1)
-        hand_out(last, nc.vector.tensor_copy, nc.scalar)
+                nc.scalar.activation(rows[t][:, c0:c1], h_ps[:], COPY, scale=-0.0625)
+                nc.scalar.activation(st_t[:, S + c0 : S + c1], h_ps[:], COPY, scale=0.0625)
+
+        out_rows = out_0.rearrange("(p t) c -> p t c", t=PACK)
+        out_words = out_1[0].rearrange("p m t -> p (m t)").bitcast(I32)
+        o = tile([P, PACK, S], F32, "o")
+
+        def step(t):
+            nc.vector.tensor_tensor(st[t][:, :S], rows[t][:].indirect(n3_sb[:]), st[t][:, S:], ADD)
+
+        step(0)
+        step(1)
+        fetched = tile([P, 2, S], F32, "fetched", tag="rows1")
+
+        def fetch(t, c0, c1):
+            nc.vector.tensor_copy(fetched[:, t % 2, c0:c1], st[t][:].indirect(entries(n4_sb, c0, c1)))
+
+        def larger(t, c0, c1):
+            nc.vector.tensor_tensor(o[:, t, c0:c1], st[t][:, c0:c1], fetched[:, t % 2, c0:c1], MAX)
+
+        for t in range(2):
+            fetch(t, 0, S)
+            step(t + 2)
+            larger(t, 0, S)
+            nc.sync.dma_start(out_rows[:, t, :], o[:, t, :])
+        (a0, a1), (b0, b1) = HALVES
+        o16 = tile([P, PACK * S], BF16, "o16")
+        out_scales = tile([P, S], U8, "out_scales")
+        words = tile([P, S], I32, "words")
+
+        def planes(c0, c1, queue):
+            nc.vector.quantize_mx(words[:, c0:c1].bitcast(FP8X4), out_scales[:, c0:c1], o16[:, PACK * c0 : PACK * c1])
+            queue.dma_start(out_words[:, c0:c1], words[:, c0:c1])
+
+        fetch(2, a0, a1)
+        fetch(3, a0, a1)
+        larger(2, a0, a1)
+        fetch(2, b0, b1)
+        larger(3, a0, a1)
+        nc.sync.dma_start(out_rows[:, 2:, a0:a1], o[:, 2:, a0:a1])
+        interleave(nc.scalar.copy, o16[:, PACK * a0 : PACK * a1], o[:, :, a0:a1])
+        fetch(3, b0, b1)
+        larger(2, b0, b1)
+        larger(3, b0, b1)
+        nc.sync.dma_start(out_rows[:, 2:, b0:b1], o[:, 2:, b0:b1])
+        mid = (b0 + b1) // 2
+        interleave(nc.scalar.copy, o16[:, PACK * b0 : PACK * mid], o[:, :, b0:mid])
+        planes(a0, a1, nc.sync)
+        interleave(nc.vector.tensor_copy, o16[:, PACK * mid : PACK * b1], o[:, :, mid:b1])
+        planes(b0, b1, nc.scalar)
         for q in range(4):
             queue = nc.scalar if q % 2 else nc.sync
             queue.dma_start(out_2[0, 4 * q : 4 * q + 4, :].bitcast(I32), out_scales[32 * q : 32 * q + 4, :].bitcast(I32))

@@ -1,6 +1,7 @@
 from contextlib import ExitStack
 
 import concourse.mybir as mybir
+from concourse.masks import make_identity
 
 K, T, S, H, G = 512, 2048, 512, 512, 2048
 FLOPS = 2 * K * H * S + 2 * H * H * S
@@ -16,6 +17,7 @@ FP4X4 = mybir.dt.float4_e2m1fn_x4
 MULT = mybir.AluOpType.mult
 ADD = mybir.AluOpType.add
 MAX = mybir.AluOpType.max
+RELU = mybir.ActivationFunctionType.Relu
 COPY = mybir.ActivationFunctionType.Copy
 
 P = 128
@@ -72,9 +74,16 @@ def tile_picked_densesumhopmx_none_po_kernel(
         for q in range(4):
             queue = nc.scalar if q < 3 else nc.gpsimd
             queue.dma_start(w1s_raw[32 * q : 32 * q + 4, :].bitcast(I32), w1_scales[0, 4 * q : 4 * q + 4, :].bitcast(I32))
+        zeros = rows[0][:, S:]
+        three_quarters = tile([P, S], F32, "three_quarters")
+        nc.scalar.activation(three_quarters[:], zeros, COPY, bias=0.75)
         for t in range(2, PACK):
-            nc.gpsimd.memset(rows[t][:, S:], 0.0)
+            nc.scalar.copy(rows[t][:, S:], zeros)
+        minus_one = tile([P, S], F32, "minus_one")
+        nc.scalar.activation(minus_one[:], zeros, COPY, bias=-1.0)
         nc.gpsimd.memset(ds_placed[:].bitcast(I32), 0)
+        identity = tile([P, P], F32, "identity")
+        make_identity(nc, identity[:])
         for e in range(2):
             nc.sync.dma_start(ds_table[e:P:16, :].bitcast(I32), d_scales[0, e:16:2, :].bitcast(I32))
         n2_sb = load_list(n2, "n2_sb")
@@ -88,12 +97,12 @@ def tile_picked_densesumhopmx_none_po_kernel(
         )
         xs = tile([P, S], U8, "xs")
         nc.vector.tensor_copy(xs[:], xs_table[:].indirect(offs_sb[:]))
-        dw_table = tile([P, G], I32, "dw_table", tag="xs_table")
+        w1s = tile([P, H], U8, "w1s", tag="xs_table")
+        nc.vector.tensor_copy(w1s[:].rearrange("p (t m) -> p t m", t=PACK), w1s_raw[:].rearrange("p (m t) -> p t m", t=PACK))
+        dw_table = tile([P, G], I32, "dw_table", tag="w1s_raw")
         nc.sync.dma_start(dw_table[:], d_words[0].rearrange("p n t -> p (n t)").bitcast(I32))
         xw = tile([P, S], U32, "xw")
         nc.vector.tensor_copy(xw[:], xw_table[:].bitcast(U32).indirect(offs_sb[:]))
-        w1s = tile([P, H], U8, "w1s")
-        nc.vector.tensor_copy(w1s[:].rearrange("p (t m) -> p t m", t=PACK), w1s_raw[:].rearrange("p (m t) -> p t m", t=PACK))
 
         for t in range(PACK):
             y_ps = psum.tile([P, S], F32, name=f"y_ps{t}", tag=f"bank{t}")
@@ -120,33 +129,32 @@ def tile_picked_densesumhopmx_none_po_kernel(
 
         zw = tile([P, S], U32, "zw")
         zs = tile([P, S], U8, "zs")
-        second = tile([P, 2, S], F32, "second")
-        z = tile([P, PACK, S], F32, "z")
+        second = [tile([P, S], F32, f"second{t}") for t in range(PACK)]
+        z = [tile([P, PACK, c1 - c0], F32, f"z{i}") for i, (c0, c1) in enumerate(HALVES)]
+        z16 = [tile([P, PACK * (c1 - c0)], BF16, f"z16_{i}") for i, (c0, c1) in enumerate(HALVES)]
 
-        def fetch_second(t, c0, c1):
-            nc.vector.tensor_scalar(second[:, t % 2, c0:c1], rows[t][:].indirect(entries(n2_sb, c0, c1)), 0.75, 0.0, MULT, ADD)
+        def fetch_second(t):
+            nc.vector.tensor_tensor(second[t][:], rows[t][:].indirect(n2_sb[:]), three_quarters[:], MULT)
 
-        def add_first(t, c0, c1):
-            nc.vector.tensor_tensor(z[:, t, c0:c1], rows[t][:].indirect(entries(n1_sb, c0, c1)), second[:, t % 2, c0:c1], ADD)
-
-        fetch_second(0, 0, S)
-        for t in range(2):
-            fetch_second(t + 1, 0, S)
-            add_first(t, 0, S)
-        z16 = []
-        for i, (c0, c1) in enumerate(HALVES):
-            fetch_second(3, c0, c1)
-            add_first(2, c0, c1)
-            add_first(3, c0, c1)
-            z16_i = tile([P, PACK * (c1 - c0)], BF16, f"z16_{i}")
-            interleave(nc.scalar.copy, z16_i[:], z[:, :, c0:c1])
-            z16.append(z16_i)
+        def add_first(t, i):
+            c0, c1 = HALVES[i]
+            nc.vector.tensor_tensor(z[i][:, t, :], rows[t][:].indirect(entries(n1_sb, c0, c1)), second[t][:, c0:c1], ADD)
 
         def quantize_z(i):
             c0, c1 = HALVES[i]
             nc.vector.quantize_mx(zw[:, c0:c1].bitcast(FP8X4), zs[:, c0:c1], z16[i][:])
 
-        dw_picked = tile([P, H], U32, "dw_picked", tag="second")
+        fetch_second(0)
+        for t in range(PACK):
+            if t + 1 < PACK:
+                fetch_second(t + 1)
+            add_first(t, 0)
+        interleave(nc.scalar.copy, z16[0][:], z[0][:])
+        for t in range(PACK):
+            add_first(t, 1)
+        interleave(nc.scalar.copy, z16[1][:], z[1][:])
+
+        dw_picked = tile([P, H], U32, "dw_picked", tag="second2")
         nc.vector.tensor_copy(dw_picked[:], dw_table[:].bitcast(U32).indirect(k1_sb[:]))
         quantize_z(0)
         dw_view = dw_picked[:].bitcast(I32).rearrange("p (m t) -> p t m", t=PACK)
@@ -154,19 +162,17 @@ def tile_picked_densesumhopmx_none_po_kernel(
         nc.vector.tensor_copy(dw_first[:], dw_view[:, 0, :])
         quantize_z(1)
         dw_rest = tile([P, PACK - 1, P], I32, "dw_rest", tag="z16_1")
-        for t in range(1, PACK):
-            nc.vector.tensor_copy(dw_rest[:, t - 1, :], dw_view[:, t, :])
+        nc.vector.tensor_copy(dw_rest[:], dw_view[:, 1:, :])
 
         st = []
         for t in range(PACK):
-            dw_t = dw_first[:] if t == 0 else dw_rest[:, t - 1, :]
             st_t = tile([P, 2 * S], F32, f"st{t}")
             st.append(st_t)
-            for i, (c0, c1) in enumerate(HALVES):
+            for i, (c0, c1) in enumerate(HALVES if t == 0 else ((0, S),)):
                 h_ps = psum.tile([P, c1 - c0], F32, name=f"h_ps{t}_{i}", tag=f"bank{t + PACK * (1 - i)}")
                 nc.tensor.matmul_mx(
                     h_ps[:],
-                    lhsT=dw_t.bitcast(FP8X4),
+                    lhsT=(dw_first[:] if t == 0 else dw_rest[:, t - 1, :]).bitcast(FP8X4),
                     lhsT_scale=ds_placed[:, P * t : P * (t + 1)],
                     rhs=zw[:, c0:c1].bitcast(FP8X4),
                     rhs_scale=zs[:, c0:c1],
@@ -178,26 +184,50 @@ def tile_picked_densesumhopmx_none_po_kernel(
 
         out_rows = out_0.rearrange("(p t) c -> p t c", t=PACK)
         out_words = out_1[0].rearrange("p m t -> p (m t)").bitcast(I32)
-        o = tile([P, PACK, S], F32, "o")
+        o = [tile([P, PACK, c1 - c0], F32, f"o{i}") for i, (c0, c1) in enumerate(HALVES)]
 
-        def step(t):
-            nc.vector.tensor_tensor(st[t][:, :S], rows[t][:].indirect(n3_sb[:]), st[t][:, S:], ADD)
+        def step(t, c0, c1):
+            nc.vector.tensor_tensor(st[t][:, c0:c1], rows[t][:].indirect(entries(n3_sb, c0, c1)), st[t][:, S + c0 : S + c1], ADD)
 
-        step(0)
-        step(1)
-        fetched = tile([P, 2, S], F32, "fetched", tag="rows1")
+        for c0, c1 in HALVES:
+            step(0, c0, c1)
+        step(1, 0, S)
+
+        def store_rows(i):
+            c0, c1 = HALVES[i]
+            nc.sync.dma_start(out_rows[:, :, c0:c1], o[i][:])
+
+        def turned_sum(n, name, *terms):
+            bank = psum.tile([P, S], F32, name=name, tag=f"bank{n}")
+            for k, term in enumerate(terms):
+                for b in range(PACK):
+                    cols = slice(P * b, P * (b + 1))
+                    first, last = k == 0 and b == 0, k == len(terms) - 1 and b == PACK - 1
+                    nc.tensor.matmul(bank[:, cols], lhsT=term[:, cols], rhs=identity[:], is_transpose=True, start=first, stop=last)
+            return bank
+
+        negated = tile([P, 2, S], F32, "negated", tag="rows1")
+        for t in range(2):
+            nc.vector.tensor_tensor(negated[:, t, :], st[t][:].indirect(n4_sb[:]), minus_one[:], MULT)
+        for t in range(2, PACK):
+            step(t, 0, S)
+        for t in range(2):
+            st_turned = tile([P, S], F32, f"st_turned{t}")
+            nc.scalar.copy(st_turned[:], turned_sum(1 + t, f"st_ps{t}", st[t][:, :S])[:])
+            excess = tile([P, S], F32, f"excess{t}")
+            nc.scalar.activation(excess[:], turned_sum(3 + t, f"gap_ps{t}", st[t][:, :S], negated[:, t, :])[:], RELU, scale=-1.0)
+            o_ps = turned_sum(5 * t, f"o_ps{t}", st_turned[:], excess[:])
+            for i, (c0, c1) in enumerate(HALVES):
+                nc.scalar.copy(o[i][:, t, :], o_ps[:, c0:c1])
+        fetched = tile([P, 2, S], F32, "fetched", tag="rows3")
 
         def fetch(t, c0, c1):
             nc.vector.tensor_copy(fetched[:, t % 2, c0:c1], st[t][:].indirect(entries(n4_sb, c0, c1)))
 
-        def larger(t, c0, c1):
-            nc.vector.tensor_tensor(o[:, t, c0:c1], st[t][:, c0:c1], fetched[:, t % 2, c0:c1], MAX)
+        def larger(t, i):
+            c0, c1 = HALVES[i]
+            nc.vector.tensor_tensor(o[i][:, t, :], st[t][:, c0:c1], fetched[:, t % 2, c0:c1], MAX)
 
-        for t in range(2):
-            fetch(t, 0, S)
-            step(t + 2)
-            larger(t, 0, S)
-            nc.sync.dma_start(out_rows[:, t, :], o[:, t, :])
         (a0, a1), (b0, b1) = HALVES
         o16 = tile([P, PACK * S], BF16, "o16")
         out_scales = tile([P, S], U8, "out_scales")
@@ -209,19 +239,19 @@ def tile_picked_densesumhopmx_none_po_kernel(
 
         fetch(2, a0, a1)
         fetch(3, a0, a1)
-        larger(2, a0, a1)
+        larger(2, 0)
+        larger(3, 0)
+        store_rows(0)
+        interleave(nc.scalar.copy, o16[:, PACK * a0 : PACK * a1], o[0][:])
         fetch(2, b0, b1)
-        larger(3, a0, a1)
-        nc.sync.dma_start(out_rows[:, 2:, a0:a1], o[:, 2:, a0:a1])
-        interleave(nc.scalar.copy, o16[:, PACK * a0 : PACK * a1], o[:, :, a0:a1])
         fetch(3, b0, b1)
-        larger(2, b0, b1)
-        larger(3, b0, b1)
-        nc.sync.dma_start(out_rows[:, 2:, b0:b1], o[:, 2:, b0:b1])
+        larger(2, 1)
+        larger(3, 1)
+        store_rows(1)
         mid = (b0 + b1) // 2
-        interleave(nc.scalar.copy, o16[:, PACK * b0 : PACK * mid], o[:, :, b0:mid])
+        interleave(nc.scalar.copy, o16[:, PACK * b0 : PACK * mid], o[1][:, :, : mid - b0])
         planes(a0, a1, nc.sync)
-        interleave(nc.vector.tensor_copy, o16[:, PACK * mid : PACK * b1], o[:, :, mid:b1])
+        interleave(nc.vector.tensor_copy, o16[:, PACK * mid : PACK * b1], o[1][:, :, mid - b0 :])
         planes(b0, b1, nc.scalar)
         for q in range(4):
             queue = nc.scalar if q % 2 else nc.sync

@@ -75,12 +75,8 @@ def tile_picked_densesumhopmx_none_po_kernel(
             queue = nc.scalar if q < 3 else nc.gpsimd
             queue.dma_start(w1s_raw[32 * q : 32 * q + 4, :].bitcast(I32), w1_scales[0, 4 * q : 4 * q + 4, :].bitcast(I32))
         zeros = rows[0][:, S:]
-        three_quarters = tile([P, S], F32, "three_quarters")
-        nc.scalar.activation(three_quarters[:], zeros, COPY, bias=0.75)
         for t in range(2, PACK):
             nc.scalar.copy(rows[t][:, S:], zeros)
-        minus_one = tile([P, S], F32, "minus_one")
-        nc.scalar.activation(minus_one[:], zeros, COPY, bias=-1.0)
         nc.gpsimd.memset(ds_placed[:].bitcast(I32), 0)
         identity = tile([P, P], F32, "identity")
         make_identity(nc, identity[:])
@@ -130,15 +126,15 @@ def tile_picked_densesumhopmx_none_po_kernel(
         zw = tile([P, S], U32, "zw")
         zs = tile([P, S], U8, "zs")
         second = [tile([P, S], F32, f"second{t}") for t in range(PACK)]
-        z = [tile([P, PACK, c1 - c0], F32, f"z{i}") for i, (c0, c1) in enumerate(HALVES)]
+        z = tile([P, 2, PACK, S // 2], F32, "z", tag="gs_sb")
         z16 = [tile([P, PACK * (c1 - c0)], BF16, f"z16_{i}") for i, (c0, c1) in enumerate(HALVES)]
 
         def fetch_second(t):
-            nc.vector.tensor_tensor(second[t][:], rows[t][:].indirect(n2_sb[:]), three_quarters[:], MULT)
+            nc.vector.tensor_scalar(second[t][:], rows[t][:].indirect(n2_sb[:]), 0.75, 0.0, MULT, ADD)
 
         def add_first(t, i):
             c0, c1 = HALVES[i]
-            nc.vector.tensor_tensor(z[i][:, t, :], rows[t][:].indirect(entries(n1_sb, c0, c1)), second[t][:, c0:c1], ADD)
+            nc.vector.tensor_tensor(z[:, i, t, :], rows[t][:].indirect(entries(n1_sb, c0, c1)), second[t][:, c0:c1], ADD)
 
         def quantize_z(i):
             c0, c1 = HALVES[i]
@@ -149,10 +145,10 @@ def tile_picked_densesumhopmx_none_po_kernel(
             if t + 1 < PACK:
                 fetch_second(t + 1)
             add_first(t, 0)
-        interleave(nc.scalar.copy, z16[0][:], z[0][:])
+        interleave(nc.scalar.copy, z16[0][:], z[:, 0])
         for t in range(PACK):
             add_first(t, 1)
-        interleave(nc.scalar.copy, z16[1][:], z[1][:])
+        interleave(nc.scalar.copy, z16[1][:], z[:, 1])
 
         dw_picked = tile([P, H], U32, "dw_picked", tag="second2")
         nc.vector.tensor_copy(dw_picked[:], dw_table[:].bitcast(U32).indirect(k1_sb[:]))
@@ -206,19 +202,17 @@ def tile_picked_densesumhopmx_none_po_kernel(
                     nc.tensor.matmul(bank[:, cols], lhsT=term[:, cols], rhs=identity[:], is_transpose=True, start=first, stop=last)
             return bank
 
-        negated = tile([P, 2, S], F32, "negated", tag="rows1")
-        for t in range(2):
-            nc.vector.tensor_tensor(negated[:, t, :], st[t][:].indirect(n4_sb[:]), minus_one[:], MULT)
+        negated = tile([P, S], F32, "negated", tag="rows1")
+        nc.vector.tensor_scalar(negated[:], st[0][:].indirect(n4_sb[:]), -1.0, 0.0, MULT, ADD)
         for t in range(2, PACK):
             step(t, 0, S)
-        for t in range(2):
-            st_turned = tile([P, S], F32, f"st_turned{t}")
-            nc.scalar.copy(st_turned[:], turned_sum(1 + t, f"st_ps{t}", st[t][:, :S])[:])
-            excess = tile([P, S], F32, f"excess{t}")
-            nc.scalar.activation(excess[:], turned_sum(3 + t, f"gap_ps{t}", st[t][:, :S], negated[:, t, :])[:], RELU, scale=-1.0)
-            o_ps = turned_sum(5 * t, f"o_ps{t}", st_turned[:], excess[:])
-            for i, (c0, c1) in enumerate(HALVES):
-                nc.scalar.copy(o[i][:, t, :], o_ps[:, c0:c1])
+        st_turned = tile([P, S], F32, "st_turned")
+        nc.scalar.copy(st_turned[:], turned_sum(1, "st_ps", st[0][:, :S])[:])
+        excess = tile([P, S], F32, "excess")
+        nc.scalar.activation(excess[:], turned_sum(2, "gap_ps", st[0][:, :S], negated[:])[:], RELU, scale=-1.0)
+        o_ps = turned_sum(3, "o_ps", st_turned[:], excess[:])
+        for i, (c0, c1) in enumerate(HALVES):
+            nc.scalar.copy(o[i][:, 0, :], o_ps[:, c0:c1])
         fetched = tile([P, 2, S], F32, "fetched", tag="rows3")
 
         def fetch(t, c0, c1):
@@ -237,7 +231,10 @@ def tile_picked_densesumhopmx_none_po_kernel(
             nc.vector.quantize_mx(words[:, c0:c1].bitcast(FP8X4), out_scales[:, c0:c1], o16[:, PACK * c0 : PACK * c1])
             queue.dma_start(out_words[:, c0:c1], words[:, c0:c1])
 
+        fetch(1, 0, S)
         fetch(2, a0, a1)
+        larger(1, 0)
+        larger(1, 1)
         fetch(3, a0, a1)
         larger(2, 0)
         larger(3, 0)

from contextlib import ExitStack

import concourse.mybir as mybir
from concourse.masks import make_identity

K, T, S, H, G = 512, 2048, 512, 512, 2048
FLOPS = 2 * K * H * S + 2 * H * H * S

F32 = mybir.dt.float32
BF16 = mybir.dt.bfloat16
I32 = mybir.dt.int32
U32 = mybir.dt.uint32
U16 = mybir.dt.uint16
U8 = mybir.dt.uint8
FP8X4 = mybir.dt.float8_e4m3fn_x4
FP4X4 = mybir.dt.float4_e2m1fn_x4
MULT = mybir.AluOpType.mult
ADD = mybir.AluOpType.add
MAX = mybir.AluOpType.max
RELU = mybir.ActivationFunctionType.Relu
COPY = mybir.ActivationFunctionType.Copy

P = 128
PACK = 4
HALVES = ((0, 256), (256, 512))


def entries(offsets, c0, c1):
    return offsets[:, c0 // 16 : c1 // 16]


def interleave(copy, dst, src):
    copy(dst.rearrange("p (c i t) -> p c t i", i=4, t=PACK), src.rearrange("p t (c i) -> p c t i", i=4))


def tile_picked_densesumhopmx_none_po_kernel(
    tc, x_words, x_scales, w1_words, w1_scales, gs, d_words, d_scales, offs, n1, n2, k1, n3, n4, out_0, out_1, out_2
):
    nc = tc.nc
    with ExitStack() as ctx:
        lists = ctx.enter_context(tc.tile_pool(name="lists", bufs=1))
        sb = ctx.enter_context(tc.tile_pool(name="sb", bufs=1))
        psum = ctx.enter_context(tc.psum_pool(name="psum", bufs=1))

        def tile(shape, dtype, name, tag=None):
            return sb.tile(shape, dtype, name=name, tag=tag or name, align_bytes=64)

        def load_list(src, name):
            offsets = lists.tile([P, S // 16], U16, name=name)
            nc.sync.dma_start(offsets[:], src)
            return offsets

        xs_table = tile([P, T], U8, "xs_table")
        w1s_raw = tile([P, H], U8, "w1s_raw")
        ds_table = tile([P, G], U8, "ds_table")
        ds_placed = tile([P, H], U8, "ds_placed")
        rows = [tile([P, 2 * S], F32, f"rows{t}") for t in range(PACK)]
        nc.vector.memset(xs_table[:].bitcast(I32), 0)
        nc.vector.memset(w1s_raw[:].bitcast(I32), 0)
        nc.vector.memset(ds_table[:].bitcast(I32), 0)
        for t in range(2):
            nc.vector.memset(rows[t][:, S:], 0.0)

        offs_sb = load_list(offs, "offs_sb")
        w1w_raw = tile([P, 2 * H], U8, "w1w_raw")
        nc.sync.dma_start(w1w_raw[:].bitcast(I32), w1_words[0].bitcast(I32))
        k1_sb = load_list(k1, "k1_sb")
        xw_table = tile([P, T], I32, "xw_table")
        nc.sync.dma_start(xw_table[:], x_words[0].rearrange("p n t -> p (n t)").bitcast(I32))
        gs_sb = tile([P, PACK], F32, "gs_sb")
        nc.gpsimd.dma_start(gs_sb[:], gs.rearrange("(p t) o -> p (t o)", t=PACK))
        for q in range(4):
            nc.scalar.dma_start(xs_table[32 * q : 32 * q + 4, :].bitcast(I32), x_scales[0, 4 * q : 4 * q + 4, :].bitcast(I32))
        for q in range(4):
            queue = nc.scalar if q < 3 else nc.gpsimd
            queue.dma_start(w1s_raw[32 * q : 32 * q + 4, :].bitcast(I32), w1_scales[0, 4 * q : 4 * q + 4, :].bitcast(I32))
        zeros = rows[0][:, S:]
        for t in range(2, PACK):
            nc.scalar.copy(rows[t][:, S:], zeros)
        nc.gpsimd.memset(ds_placed[:].bitcast(I32), 0)
        identity = tile([P, P], F32, "identity")
        make_identity(nc, identity[:])
        for e in range(2):
            nc.sync.dma_start(ds_table[e:P:16, :].bitcast(I32), d_scales[0, e:16:2, :].bitcast(I32))
        n2_sb = load_list(n2, "n2_sb")
        n1_sb = load_list(n1, "n1_sb")
        n3_sb = load_list(n3, "n3_sb")
        n4_sb = load_list(n4, "n4_sb")

        w1w = tile([P, 2 * H], U8, "w1w")
        nc.vector.tensor_copy(
            w1w[:].rearrange("p (t m b) -> p t m b", t=PACK, b=2), w1w_raw[:].rearrange("p (m t b) -> p t m b", t=PACK, b=2)
        )
        xs = tile([P, S], U8, "xs")
        nc.vector.tensor_copy(xs[:], xs_table[:].indirect(offs_sb[:]))
        w1s = tile([P, H], U8, "w1s", tag="xs_table")
        nc.vector.tensor_copy(w1s[:].rearrange("p (t m) -> p t m", t=PACK), w1s_raw[:].rearrange("p (m t) -> p t m", t=PACK))
        dw_table = tile([P, G], I32, "dw_table", tag="w1s_raw")
        nc.sync.dma_start(dw_table[:], d_words[0].rearrange("p n t -> p (n t)").bitcast(I32))
        xw = tile([P, S], U32, "xw")
        nc.vector.tensor_copy(xw[:], xw_table[:].bitcast(U32).indirect(offs_sb[:]))

        for t in range(PACK):
            y_ps = psum.tile([P, S], F32, name=f"y_ps{t}", tag=f"bank{t}")
            nc.tensor.matmul_mx(
                y_ps[:],
                lhsT=w1w[:, 2 * P * t : 2 * P * (t + 1)].bitcast(FP4X4),
                lhsT_scale=w1s[:, P * t : P * (t + 1)],
                rhs=xw[:].bitcast(FP8X4),
                rhs_scale=xs[:],
                start=True,
                stop=True,
            )
            nc.scalar.activation(rows[t][:, :S], y_ps[:], COPY, scale=gs_sb[:, t : t + 1])

        ds_picked = tile([P, H], U8, "ds_picked", tag="xw_table")
        nc.vector.tensor_copy(ds_picked[:], ds_table[:].indirect(k1_sb[:]))
        ds_dealt = tile([P, H], U8, "ds_dealt")
        nc.vector.tensor_copy(
            ds_dealt[:].rearrange("p (t m) -> p t m", t=PACK), ds_picked[:].rearrange("p (m t) -> p t m", t=PACK)
        )
        for odd in range(2):
            for e in range(2):
                nc.sync.dma_start(ds_placed[2 * odd + e : P : 32, :].bitcast(I32), ds_dealt[16 * odd + e : P : 32, :].bitcast(I32))

        zw = tile([P, S], U32, "zw")
        zs = tile([P, S], U8, "zs")
        second = [tile([P, S], F32, f"second{t}") for t in range(PACK)]
        z = tile([P, 2, PACK, S // 2], F32, "z", tag="gs_sb")
        z16 = [tile([P, PACK * (c1 - c0)], BF16, f"z16_{i}") for i, (c0, c1) in enumerate(HALVES)]

        def fetch_second(t):
            nc.vector.tensor_scalar(second[t][:], rows[t][:].indirect(n2_sb[:]), 0.75, 0.0, MULT, ADD)

        def add_first(t, i):
            c0, c1 = HALVES[i]
            nc.vector.tensor_tensor(z[:, i, t, :], rows[t][:].indirect(entries(n1_sb, c0, c1)), second[t][:, c0:c1], ADD)

        def quantize_z(i):
            c0, c1 = HALVES[i]
            nc.vector.quantize_mx(zw[:, c0:c1].bitcast(FP8X4), zs[:, c0:c1], z16[i][:])

        fetch_second(0)
        for t in range(PACK):
            if t + 1 < PACK:
                fetch_second(t + 1)
            add_first(t, 0)
        interleave(nc.scalar.copy, z16[0][:], z[:, 0])
        for t in range(PACK):
            add_first(t, 1)
        interleave(nc.scalar.copy, z16[1][:], z[:, 1])

        dw_picked = tile([P, H], U32, "dw_picked", tag="second2")
        nc.vector.tensor_copy(dw_picked[:], dw_table[:].bitcast(U32).indirect(k1_sb[:]))
        quantize_z(0)
        dw_view = dw_picked[:].bitcast(I32).rearrange("p (m t) -> p t m", t=PACK)
        dw_first = tile([P, P], I32, "dw_first")
        nc.vector.tensor_copy(dw_first[:], dw_view[:, 0, :])
        quantize_z(1)
        dw_rest = tile([P, PACK - 1, P], I32, "dw_rest", tag="z16_1")
        nc.vector.tensor_copy(dw_rest[:], dw_view[:, 1:, :])

        st = []
        for t in range(PACK):
            st_t = tile([P, 2 * S], F32, f"st{t}")
            st.append(st_t)
            for i, (c0, c1) in enumerate(HALVES if t == 0 else ((0, S),)):
                h_ps = psum.tile([P, c1 - c0], F32, name=f"h_ps{t}_{i}", tag=f"bank{t + PACK * (1 - i)}")
                nc.tensor.matmul_mx(
                    h_ps[:],
                    lhsT=(dw_first[:] if t == 0 else dw_rest[:, t - 1, :]).bitcast(FP8X4),
                    lhsT_scale=ds_placed[:, P * t : P * (t + 1)],
                    rhs=zw[:, c0:c1].bitcast(FP8X4),
                    rhs_scale=zs[:, c0:c1],
                    start=True,
                    stop=True,
                )
                nc.scalar.activation(rows[t][:, c0:c1], h_ps[:], COPY, scale=-0.0625)
                nc.scalar.activation(st_t[:, S + c0 : S + c1], h_ps[:], COPY, scale=0.0625)

        out_rows = out_0.rearrange("(p t) c -> p t c", t=PACK)
        out_words = out_1[0].rearrange("p m t -> p (m t)").bitcast(I32)
        o = [tile([P, PACK, c1 - c0], F32, f"o{i}") for i, (c0, c1) in enumerate(HALVES)]

        def step(t, c0, c1):
            nc.vector.tensor_tensor(st[t][:, c0:c1], rows[t][:].indirect(entries(n3_sb, c0, c1)), st[t][:, S + c0 : S + c1], ADD)

        for c0, c1 in HALVES:
            step(0, c0, c1)
        step(1, 0, S)

        def store_rows(i):
            c0, c1 = HALVES[i]
            nc.sync.dma_start(out_rows[:, :, c0:c1], o[i][:])

        def turned_sum(n, name, *terms):
            bank = psum.tile([P, S], F32, name=name, tag=f"bank{n}")
            for k, term in enumerate(terms):
                for b in range(PACK):
                    cols = slice(P * b, P * (b + 1))
                    first, last = k == 0 and b == 0, k == len(terms) - 1 and b == PACK - 1
                    nc.tensor.matmul(bank[:, cols], lhsT=term[:, cols], rhs=identity[:], is_transpose=True, start=first, stop=last)
            return bank

        negated = tile([P, S], F32, "negated", tag="rows1")
        nc.vector.tensor_scalar(negated[:], st[0][:].indirect(n4_sb[:]), -1.0, 0.0, MULT, ADD)
        for t in range(2, PACK):
            step(t, 0, S)
        st_turned = tile([P, S], F32, "st_turned")
        nc.scalar.copy(st_turned[:], turned_sum(1, "st_ps", st[0][:, :S])[:])
        excess = tile([P, S], F32, "excess")
        nc.scalar.activation(excess[:], turned_sum(2, "gap_ps", st[0][:, :S], negated[:])[:], RELU, scale=-1.0)
        o_ps = turned_sum(3, "o_ps", st_turned[:], excess[:])
        for i, (c0, c1) in enumerate(HALVES):
            nc.scalar.copy(o[i][:, 0, :], o_ps[:, c0:c1])
        fetched = tile([P, 2, S], F32, "fetched", tag="rows3")

        def fetch(t, c0, c1):
            nc.vector.tensor_copy(fetched[:, t % 2, c0:c1], st[t][:].indirect(entries(n4_sb, c0, c1)))

        def larger(t, i):
            c0, c1 = HALVES[i]
            nc.vector.tensor_tensor(o[i][:, t, :], st[t][:, c0:c1], fetched[:, t % 2, c0:c1], MAX)

        (a0, a1), (b0, b1) = HALVES
        o16 = tile([P, PACK * S], BF16, "o16")
        out_scales = tile([P, S], U8, "out_scales")
        words = tile([P, S], I32, "words")

        def planes(c0, c1, queue):
            nc.vector.quantize_mx(words[:, c0:c1].bitcast(FP8X4), out_scales[:, c0:c1], o16[:, PACK * c0 : PACK * c1])
            queue.dma_start(out_words[:, c0:c1], words[:, c0:c1])

        fetch(1, 0, S)
        fetch(2, a0, a1)
        larger(1, 0)
        larger(1, 1)
        fetch(3, a0, a1)
        larger(2, 0)
        larger(3, 0)
        store_rows(0)
        interleave(nc.scalar.copy, o16[:, PACK * a0 : PACK * a1], o[0][:])
        fetch(2, b0, b1)
        fetch(3, b0, b1)
        larger(2, 1)
        larger(3, 1)
        store_rows(1)
        mid = (b0 + b1) // 2
        interleave(nc.scalar.copy, o16[:, PACK * b0 : PACK * mid], o[1][:, :, : mid - b0])
        planes(a0, a1, nc.sync)
        interleave(nc.vector.tensor_copy, o16[:, PACK * mid : PACK * b1], o[1][:, :, mid - b0 :])
        planes(b0, b1, nc.scalar)
        for q in range(4):
            queue = nc.scalar if q % 2 else nc.sync
            queue.dma_start(out_2[0, 4 * q : 4 * q + 4, :].bitcast(I32), out_scales[32 * q : 32 * q + 4, :].bitcast(I32))
